import numpy as np
import ml_dtypes


def mxq(x, axis, fmt="e4m3"):
    dtype, down = {"e4m3": (ml_dtypes.float8_e4m3fn, 7), "e5m2": (ml_dtypes.float8_e5m2, 14)}[fmt]
    v = np.moveaxis(np.asarray(x, np.float32).astype(ml_dtypes.bfloat16).astype(np.float64), axis, -1)
    blocks = v.reshape(v.shape[:-1] + (-1, 32))
    amax = np.abs(blocks).max(-1, keepdims=True)
    byte = np.maximum(np.where(amax > 0, np.frexp(amax)[1] - 1 + 127, 0) - down, 1)
    scale = np.exp2(byte - 127.0)
    codes = (blocks / scale).astype(np.float32).astype(dtype).astype(np.float64)
    return np.moveaxis((codes * scale).reshape(v.shape), -1, axis)


WIDE = False


def mx_kscale(k):
    if not WIDE:
        return np.ones(k)
    levels = np.array([10, -10, 5, -5, 0])
    if k % 512:
        return np.exp2(np.random.permutation(np.resize(levels, k // 32))).repeat(32)
    a = np.empty((k // 512, 16))
    for p in range(k // 512):
        a[p, :8] = np.random.permutation(np.resize(levels, 8))
        for g in range(8):
            far = levels[np.abs(levels - a[p, g]) >= 10]
            a[p, g + 8] = far[np.random.randint(len(far))]
    return np.exp2(a.ravel()).repeat(32)


def f64(x):
    return np.asarray(x).astype(np.float64)


def striped(idx):
    return np.tile(np.asarray(idx).reshape(-1, 16).T, (8, 1)).astype(np.uint16)


def unstriped(offs):
    return offs[:16].T.reshape(-1).astype(np.int64)


E2M1 = np.array([0.0, 0.5, 1.0, 1.5, 2.0, 3.0, 4.0, 6.0, -0.0, -0.5, -1.0, -1.5, -2.0, -3.0, -4.0, -6.0])


def pack_weight(w, fmt):
    k, n = w.shape
    w = f64(np.asarray(w, np.float32).astype(ml_dtypes.bfloat16)).reshape(k // 32, 32, n)
    amax = np.abs(w).max(1)
    if fmt == "e4m3":
        byte = np.frexp(amax)[1] - 1 + 127 - 7
    else:
        mant, ex = np.frexp(amax / 6.0)
        byte = np.where(mant > 0.5, ex, ex - 1) + 127
    byte = np.clip(np.where(amax > 0, byte, 1), 1, 254)
    scaled = (w * np.exp2(127.0 - byte)[:, None, :]).reshape(k, n).astype(np.float32)
    by_word = np.ascontiguousarray(scaled.reshape(k // 512, 128, 4, n).transpose(0, 1, 3, 2))
    if fmt == "e4m3":
        words = by_word.astype(ml_dtypes.float8_e4m3fn).view(np.uint8)
    else:
        c = by_word.astype(ml_dtypes.float4_e2m1fn).view(np.uint8) & 0xF
        words = (c[..., 0::2] | (c[..., 1::2] << 4)).reshape(k // 512, 128, 2 * n)
    return np.ascontiguousarray(words), np.ascontiguousarray(byte.astype(np.uint8).reshape(k // 512, 16, n))


def unpack_weight(words, scales, fmt):
    g, _, n = scales.shape
    words = np.ascontiguousarray(words).reshape(g, 128, n, -1)
    if fmt == "e4m3":
        vals = words.view(ml_dtypes.float8_e4m3fn).astype(np.float64)
    else:
        nib = np.empty((g, 128, n, 4), np.uint8)
        nib[..., 0::2] = words & 0xF
        nib[..., 1::2] = words >> 4
        vals = E2M1[nib]
    vals = vals * np.repeat(np.exp2(scales.astype(np.float64) - 127.0), 8, axis=1)[..., None]
    return vals.transpose(0, 1, 3, 2).reshape(g * 512, n)


B, N, T, D, DV, NQ = 1, 1024, 2048, 512, 256, 256


def setup_inputs():
    n = np.random.standard_normal
    idx = np.random.permutation(T)[:B * N]
    s = mx_kscale(D)[:, None]
    u = np.ones(T)
    u[idx] = mx_kscale(B * N)
    r = np.random.uniform(0.5, 2.0, T)
    k = n((D, T)) / s
    v = n((DV, T)) / (u * r)
    kp = pack_weight(k, "e4m3")
    return {
        "qT": (n((B, D, NQ)) * s * (1.00 / np.sqrt(D))).astype(np.float32),
        "k_words": kp[0],
        "k_scales": kp[1],
        "vT": v.astype(np.float32),
        "vs": np.tile(u * r, (128, 1)).astype(np.float32),
        "kb": np.tile(n(T), (128, 1)).astype(np.float32),
        "sink": (2.0 + 3.0 * n((B, NQ, 1))).astype(np.float32),
        "offs": striped(idx),
    }


def reference(qT, k_words, k_scales, vT, vs, kb, sink, offs):
    idx = unstriped(offs)
    k = unpack_weight(k_words, k_scales, "e4m3")
    v = f64(vT)
    pick = lambda x: x[:, idx].reshape(x.shape[0], B, N).transpose(1, 0, 2)
    q = f64(qT)
    score = mxq(q, 1, "e4m3").transpose(0, 2, 1) @ pick(k)
    score = score + pick(f64(kb))[:, :1, :]
    m = np.maximum(score.max(-1, keepdims=True), f64(sink))
    p = np.exp(score - m)
    total = p.sum(-1, keepdims=True) + np.exp(f64(sink) - m)
    w = p * pick(f64(vs))[:, :1, :]
    y = mxq(w, 2, "e4m3") @ mxq(pick(v).transpose(0, 2, 1), 1, "e4m3")
    y = y / total
    return y

@@ -1,0 +1,217 @@
+from contextlib import ExitStack
+
+import concourse.mybir as mybir
+from concourse.masks import make_identity
+
+F32 = mybir.dt.float32
+BF16 = mybir.dt.bfloat16
+I32 = mybir.dt.int32
+U32 = mybir.dt.uint32
+U16 = mybir.dt.uint16
+U8 = mybir.dt.uint8
+FP8X4 = mybir.dt.float8_e4m3fn_x4
+ALU = mybir.AluOpType
+ACT = mybir.ActivationFunctionType
+
+P = 128
+PACK = 4
+PASS = P * PACK
+N, T, D, DV, NQ = 1024, 2048, 512, 256, 256
+PASSES = N // PASS
+Q_TILES = NQ // P
+V_HALVES = DV // P
+COLS = PASS // 16
+ROW = P - 1
+LAST = (V_HALVES - 1, PASSES - 1)
+
+FLOPS = 2 * NQ * N * D + 2 * NQ * N * DV
+BYTES = 4 * D * NQ + D * T + 16 * T + 4 * DV * T + 2 * 4 * T + 4 * NQ + 2 * P * N // 16 + 4 * NQ * DV
+
+
+def tile_attend_soft_sink_kb_topkq256n1024t2048_kernel(tc, qT, k_words, k_scales, vT, vs, kb, sink, offs, out):
+    nc = tc.nc
+    with ExitStack() as ctx:
+        sb = ctx.enter_context(tc.tile_pool(name="sb", bufs=1))
+        ps = ctx.enter_context(tc.psum_pool(name="ps", bufs=1))
+
+        def bank(b, name):
+            return ps.tile([P, PASS], F32, name=name, tag="bank%d" % b)
+
+        offsets = sb.tile([P, N // 16], U16, name="offsets")
+        nc.sync.dma_start(offsets[:], offs)
+
+        def listed(window, a):
+            return window.indirect(offsets[:, a * COLS : (a + 1) * COLS])
+
+        ks_pool = sb.tile([P, T], U8, name="ks_pool", align_bytes=64)
+        kb_pool = sb.tile([P, T], F32, name="kb_pool")
+        vs_pool = sb.tile([P, T], F32, name="vs_pool")
+        nc.scalar.dma_start(kb_pool[ROW:P, :], kb[0:1, :])
+        nc.vector.memset(kb_pool[0:ROW, :], 0.0)
+        for quad in range(4):
+            nc.sync.dma_start(
+                ks_pool[32 * quad : 32 * (quad + 1), :].bitcast(I32),
+                k_scales[0, 4 * quad : 4 * quad + 4, :].bitcast(I32).unsqueeze(0).to_broadcast([8, 4, T // 4]),
+            )
+        q_raw = sb.tile([P, PACK, NQ], F32, name="q_raw")
+        nc.sync.dma_start(q_raw[:], qT[0].rearrange("(p j) w -> p j w", j=PACK))
+        kw_pool = sb.tile([P, T], I32, name="kw_pool", align_bytes=64)
+        nc.sync.dma_start(kw_pool[:], k_words[0].rearrange("p n t -> p (n t)").bitcast(I32))
+        nc.sync.dma_start(vs_pool[ROW:P, :], vs[0:1, :])
+        sink_col = sb.tile([P, Q_TILES], F32, name="sink_col")
+        with nc.allow_non_contiguous_dma(reason="one sink a query row, one query row a partition"):
+            nc.sync.dma_start(sink_col[:], sink[0].rearrange("(i p) o -> p (i o)", p=P))
+        v_pool = [sb.tile([P, T], F32, name="v_pool%d" % h) for h in range(V_HALVES)]
+        for h in range(V_HALVES):
+            nc.sync.dma_start(v_pool[h][:], vT[h * P : (h + 1) * P, :])
+
+        ident = sb.tile([P, P], F32, name="ident")
+        make_identity(nc, ident[:])
+        for c in range(0, T, PASS):
+            nc.gpsimd.memset(vs_pool[0:ROW, c : c + PASS], 0.0)
+
+        ks_g = sb.tile([P, N], U8, name="ks_g", align_bytes=64)
+        nc.vector.tensor_copy(ks_g[:], ks_pool[:].indirect(offsets[:]))
+
+        kb_col = sb.tile([P, PASSES, PACK], F32, name="kb_col")
+        for a in range(PASSES):
+            kb_g = sb.tile([P, PASS], F32, name="kb_g%d" % a)
+            nc.scalar.activation(kb_g[:], listed(kb_pool[:], a), ACT.Copy)
+            turned = bank(4 + a, "kb_turned%d" % a)
+            for j in range(PACK):
+                nc.tensor.transpose(turned[:, j * P : (j + 1) * P], kb_g[:, j * P : (j + 1) * P], ident[:])
+            nc.vector.tensor_copy(kb_col[:, a, :], turned[:, ROW:PASS:P])
+
+        q_in = sb.tile([P, NQ, PACK], BF16, name="q_in", align_bytes=64)
+        nc.vector.tensor_copy(
+            q_in[:].rearrange("p (c i) t -> p c t i", i=4),
+            q_raw[:].rearrange("p t (c i) -> p c t i", i=4),
+        )
+        q_codes = sb.tile([P, NQ], U32, name="q_codes", align_bytes=64)
+        q_scales = sb.tile([P, NQ], U8, name="q_scales", align_bytes=64)
+        nc.vector.quantize_mx(out=q_codes[:].bitcast(FP8X4), scales=q_scales[:], in_=q_in[:].rearrange("p w t -> p (w t)"))
+
+        vs_g = sb.tile([P, N], F32, name="vs_g")
+        nc.scalar.activation(vs_g[:], vs_pool[:].indirect(offsets[:]), ACT.Copy)
+        vs_col = [sb.tile([P, PACK], F32, name="vs_col%d" % a) for a in range(PASSES)]
+        for a in range(PASSES):
+            nc.scalar.dma_start(vs_col[a][:], vs_g[ROW:P, a * PASS : (a + 1) * PASS])
+
+        score_t = {}
+        for a in range(PASSES):
+            kw_g = sb.tile([P, PASS], U32, name="kw_g%d" % a, align_bytes=64)
+            nc.vector.tensor_copy(kw_g[:], listed(kw_pool[:].bitcast(U32), a))
+            for i in range(Q_TILES):
+                score_t[i, a] = bank(2 * i + a, "score_t%d%d" % (i, a))
+                for j in range(PACK):
+                    nc.tensor.matmul_mx(
+                        out=score_t[i, a][:, j * P : (j + 1) * P],
+                        lhsT=kw_g[:, j * P : (j + 1) * P].bitcast(FP8X4),
+                        lhsT_scale=ks_g[:, a * PASS + j * P : a * PASS + (j + 1) * P],
+                        rhs=q_codes[:, i * P : (i + 1) * P].bitcast(FP8X4),
+                        rhs_scale=q_scales[:, i * P : (i + 1) * P],
+                        start=True,
+                        stop=True,
+                    )
+
+        v_g = {}
+        for h in range(V_HALVES):
+            for a in range(PASSES):
+                if (h, a) != LAST:
+                    v_g[h, a] = sb.tile([P, PASS], BF16, name="v_g%d%d" % (h, a))
+                    nc.scalar.activation(v_g[h, a][:], listed(v_pool[h][:], a), ACT.Copy)
+
+        score = {}
+        for i in range(Q_TILES):
+            for a in range(PASSES):
+                biased = sb.tile([P, PACK, P], F32, name="biased%d%d" % (i, a))
+                nc.vector.tensor_tensor(
+                    biased[:],
+                    score_t[i, a][:].rearrange("s (j q) -> s j q", j=PACK),
+                    kb_col[:, a, :].unsqueeze(2).to_broadcast([P, PACK, P]),
+                    ALU.add,
+                )
+                score[i, a] = bank(4 + 2 * i + a, "score%d%d" % (i, a))
+                for j in range(PACK):
+                    nc.tensor.transpose(score[i, a][:, j * P : (j + 1) * P], biased[:, j, :], ident[:])
+
+        weights, sums = [], []
+        for i in range(Q_TILES):
+            neg = sb.tile([P, N + 1], F32, name="neg%d" % i)
+            nc.gpsimd.tensor_scalar(neg[:, N : N + 1], sink_col[:, i : i + 1], -1.0, 0.0, ALU.mult, ALU.add)
+            least = neg[:, N : N + 1]
+            for a in range(PASSES):
+                running = sb.tile([P, 1], F32, name="least%d%d" % (i, a), tag="least%d%d" % (i, a))
+                nc.vector.tensor_scalar(
+                    neg[:, a * PASS : (a + 1) * PASS].rearrange("q (t s) -> q t s", t=PACK),
+                    score[i, a][:].rearrange("q (s t) -> q t s", t=PACK),
+                    -1.0,
+                    least,
+                    ALU.mult,
+                    ALU.min,
+                    accum_out=running[:],
+                )
+                least = running[:]
+            p = sb.tile([P, N + 1], F32, name="p%d" % i)
+            part = sb.tile([P, PASSES], F32, name="part%d" % i)
+            for a in range(PASSES):
+                cols = slice(a * PASS, (a + 1) * PASS + (1 if a == PASSES - 1 else 0))
+                nc.scalar.activation(p[:, cols], neg[:, cols], ACT.Exp, bias=least, scale=-1.0, accum_out=part[:, a : a + 1])
+            weights.append(p)
+            sums.append(part)
+
+        v_g[LAST] = sb.tile([P, PASS], BF16, name="v_g_last", tag="least10")
+        nc.vector.tensor_copy(v_g[LAST][:], listed(v_pool[LAST[0]][:], LAST[1]))
+
+        v_codes, v_scales = [], []
+        for a in range(PASSES):
+            turned = bank(a, "v_turned%d" % a)
+            for h in range(V_HALVES):
+                words = v_g[h, a][:].bitcast(F32)
+                for u in range(2):
+                    k = 2 * h + u
+                    nc.tensor.transpose(turned[:, k * P : (k + 1) * P], words[:, u : 2 * P : 2], ident[:])
+            v_in = sb.tile([P, DV * PACK], BF16, name="v_in%d" % a, align_bytes=64)
+            nc.scalar.copy(
+                v_in[:].bitcast(F32).rearrange("s (h e u) -> s h e u", h=V_HALVES, u=2),
+                turned[:].rearrange("s (h u e) -> s h e u", h=V_HALVES, u=2),
+            )
+            codes = sb.tile([P, DV], U32, name="v_codes%d" % a, align_bytes=64)
+            scales = sb.tile([P, DV], U8, name="v_scales%d" % a, align_bytes=64)
+            nc.vector.quantize_mx(out=codes[:].bitcast(FP8X4), scales=scales[:], in_=v_in[:])
+            v_codes.append(codes)
+            v_scales.append(scales)
+
+        for i in range(Q_TILES):
+            acc = bank(6 + i, "acc%d" % i)
+            for a in range(PASSES):
+                turned = bank(2 + 2 * i + a, "p_turned%d%d" % (i, a))
+                for t in range(PACK):
+                    c0 = a * PASS + t * P
+                    nc.tensor.transpose(turned[:, t * P : (t + 1) * P], weights[i][:, c0 : c0 + P], ident[:])
+                w_in = sb.tile([P, P, PACK], BF16, name="w_in%d%d" % (i, a), align_bytes=64)
+                nc.vector.tensor_tensor(
+                    w_in[:],
+                    turned[:].rearrange("s (t q) -> s q t", t=PACK),
+                    vs_col[a][:].unsqueeze(1).to_broadcast([P, P, PACK]),
+                    ALU.mult,
+                )
+                w_codes = sb.tile([P, P], U32, name="w_codes%d%d" % (i, a), align_bytes=64)
+                w_scales = sb.tile([P, P], U8, name="w_scales%d%d" % (i, a), align_bytes=64)
+                nc.vector.quantize_mx(out=w_codes[:].bitcast(FP8X4), scales=w_scales[:], in_=w_in[:].rearrange("s q t -> s (q t)"))
+                nc.tensor.matmul_mx(
+                    out=acc[:, 0:DV],
+                    lhsT=w_codes[:].bitcast(FP8X4),
+                    lhsT_scale=w_scales[:],
+                    rhs=v_codes[a][:].bitcast(FP8X4),
+                    rhs_scale=v_scales[a][:],
+                    start=(a == 0),
+                    stop=(a == PASSES - 1),
+                )
+            total = sb.tile([P, 1], F32, name="total%d" % i)
+            nc.vector.tensor_tensor(total[:], sums[i][:, 0:1], sums[i][:, 1:2], ALU.add)
+            inverse = sb.tile([P, 1], F32, name="inverse%d" % i)
+            nc.vector.reciprocal(inverse[:], total[:])
+            result = sb.tile([P, DV], F32, name="result%d" % i)
+            nc.scalar.activation(result[:], acc[:, 0:DV], ACT.Copy, scale=inverse[:])
+            nc.sync.dma_start(out[0, i * P : (i + 1) * P, :], result[:])

@@ -22,7 +22,6 @@ Q_TILES = NQ // P
 V_HALVES = DV // P
 COLS = PASS // 16
 ROW = P - 1
-LAST = (V_HALVES - 1, PASSES - 1)
 
 FLOPS = 2 * NQ * N * D + 2 * NQ * N * DV
 BYTES = 4 * D * NQ + D * T + 16 * T + 4 * DV * T + 2 * 4 * T + 4 * NQ + 2 * P * N // 16 + 4 * NQ * DV
@@ -37,6 +36,12 @@ def tile_attend_soft_sink_kb_topkq256n1024t2048_kernel(tc, qT, k_words, k_scales
         def bank(b, name):
             return ps.tile([P, PASS], F32, name=name, tag="bank%d" % b)
 
+        warm = sb.tile([P, 2], F32, name="warm")
+        nc.gpsimd.memset(warm[:, 0:1], 0.0)
+        nc.scalar.activation(warm[:, 1:2], warm[:, 0:1], ACT.Exp)
+        ident = sb.tile([P, P], F32, name="ident")
+        make_identity(nc, ident[:])
+
         offsets = sb.tile([P, N // 16], U16, name="offsets")
         nc.sync.dma_start(offsets[:], offs)
 
@@ -46,172 +51,195 @@ def tile_attend_soft_sink_kb_topkq256n1024t2048_kernel(tc, qT, k_words, k_scales
         ks_pool = sb.tile([P, T], U8, name="ks_pool", align_bytes=64)
         kb_pool = sb.tile([P, T], F32, name="kb_pool")
         vs_pool = sb.tile([P, T], F32, name="vs_pool")
-        nc.scalar.dma_start(kb_pool[ROW:P, :], kb[0:1, :])
-        nc.vector.memset(kb_pool[0:ROW, :], 0.0)
+        nc.vector.memset(kb_pool[0:ROW, 0 : T // 2 - 1], 0.0)
+        nc.vector.memset(kb_pool[0:ROW, T // 2 - 1 : T], 0.0)
+        nc.gpsimd.memset(vs_pool[0:ROW, :], 0.0)
         for quad in range(4):
             nc.sync.dma_start(
                 ks_pool[32 * quad : 32 * (quad + 1), :].bitcast(I32),
                 k_scales[0, 4 * quad : 4 * quad + 4, :].bitcast(I32).unsqueeze(0).to_broadcast([8, 4, T // 4]),
             )
-        q_raw = sb.tile([P, PACK, NQ], F32, name="q_raw")
-        nc.sync.dma_start(q_raw[:], qT[0].rearrange("(p j) w -> p j w", j=PACK))
-        kw_pool = sb.tile([P, T], I32, name="kw_pool", align_bytes=64)
-        nc.sync.dma_start(kw_pool[:], k_words[0].rearrange("p n t -> p (n t)").bitcast(I32))
+        nc.sync.dma_start(kb_pool[ROW:P, :], kb[0:1, :])
         nc.sync.dma_start(vs_pool[ROW:P, :], vs[0:1, :])
-        sink_col = sb.tile([P, Q_TILES], F32, name="sink_col")
-        with nc.allow_non_contiguous_dma(reason="one sink a query row, one query row a partition"):
-            nc.sync.dma_start(sink_col[:], sink[0].rearrange("(i p) o -> p (i o)", p=P))
-        v_pool = [sb.tile([P, T], F32, name="v_pool%d" % h) for h in range(V_HALVES)]
+        kw_pool = sb.tile([P, T], I32, name="kw_pool", tag="kw_pool", align_bytes=64)
+        nc.sync.dma_start(kw_pool[:], k_words[0].rearrange("p n t -> p (n t)").bitcast(I32))
+        q_raw = sb.tile([P, PACK, NQ], F32, name="q_raw", tag="q_raw", align_bytes=64)
+        nc.sync.dma_start(q_raw[:], qT[0].rearrange("(p j) w -> p j w", j=PACK))
+        score = [sb.tile([P, N + 1], F32, name="score%d" % i, tag="score%d" % i, align_bytes=64) for i in range(Q_TILES)]
+        for i in range(Q_TILES):
+            nc.sync.dma_start(score[i][:, N : N + 1], sink[0, i * P : (i + 1) * P, :])
+        v_pool = [sb.tile([P, T], F32, name="v_pool%d" % h, tag="v_pool%d" % h) for h in range(V_HALVES)]
         for h in range(V_HALVES):
             nc.sync.dma_start(v_pool[h][:], vT[h * P : (h + 1) * P, :])
 
-        ident = sb.tile([P, P], F32, name="ident")
-        make_identity(nc, ident[:])
-        for c in range(0, T, PASS):
-            nc.gpsimd.memset(vs_pool[0:ROW, c : c + PASS], 0.0)
 
         ks_g = sb.tile([P, N], U8, name="ks_g", align_bytes=64)
         nc.vector.tensor_copy(ks_g[:], ks_pool[:].indirect(offsets[:]))
 
-        kb_col = sb.tile([P, PASSES, PACK], F32, name="kb_col")
+        kb_turned = {}
         for a in range(PASSES):
-            kb_g = sb.tile([P, PASS], F32, name="kb_g%d" % a)
+            kb_g = sb.tile([P, PASS], F32, name="kb_g%d" % a, tag="kb_g%d" % a)
             nc.scalar.activation(kb_g[:], listed(kb_pool[:], a), ACT.Copy)
-            turned = bank(4 + a, "kb_turned%d" % a)
+            kb_turned[a] = bank(a, "kb_turned%d" % a)
             for j in range(PACK):
-                nc.tensor.transpose(turned[:, j * P : (j + 1) * P], kb_g[:, j * P : (j + 1) * P], ident[:])
-            nc.vector.tensor_copy(kb_col[:, a, :], turned[:, ROW:PASS:P])
+                nc.tensor.transpose(kb_turned[a][:, j * P : (j + 1) * P], kb_g[:, j * P : (j + 1) * P], ident[:])
 
-        q_in = sb.tile([P, NQ, PACK], BF16, name="q_in", align_bytes=64)
+        vs_g = sb.tile([P, N], F32, name="vs_g", tag="kb_g0")
+        nc.scalar.activation(vs_g[:], vs_pool[:].indirect(offsets[:]), ACT.Copy)
+        vs_col = {}
+        for a in range(PASSES):
+            vs_col[a] = sb.tile([P, PACK], F32, name="vs_col%d" % a, tag="vs_col%d" % a, align_bytes=64)
+            nc.sync.dma_start(vs_col[a][:], vs_g[ROW:P, a * PASS : (a + 1) * PASS])
+
+        kw_g = {}
+
+        def gather_keys(a, tag):
+            kw_g[a] = sb.tile([P, PASS], U32, name="kw_g%d" % a, tag=tag, align_bytes=64)
+            nc.vector.tensor_copy(kw_g[a][:], listed(kw_pool[:].bitcast(U32), a))
+
+        gather_keys(0, "kw_g0")
+        q_in = sb.tile([P, NQ, PACK], BF16, name="q_in", tag="q_in", align_bytes=64)
         nc.vector.tensor_copy(
             q_in[:].rearrange("p (c i) t -> p c t i", i=4),
             q_raw[:].rearrange("p t (c i) -> p c t i", i=4),
         )
+        kb_col = sb.tile([P, PASSES, PACK], F32, name="kb_col", tag="q_raw", align_bytes=64)
+        for a in range(PASSES):
+            nc.vector.tensor_copy(kb_col[:, a, :], kb_turned[a][:, ROW:PASS:P])
         q_codes = sb.tile([P, NQ], U32, name="q_codes", align_bytes=64)
         q_scales = sb.tile([P, NQ], U8, name="q_scales", align_bytes=64)
         nc.vector.quantize_mx(out=q_codes[:].bitcast(FP8X4), scales=q_scales[:], in_=q_in[:].rearrange("p w t -> p (w t)"))
+        gather_keys(1, "q_in")
 
-        vs_g = sb.tile([P, N], F32, name="vs_g")
-        nc.scalar.activation(vs_g[:], vs_pool[:].indirect(offsets[:]), ACT.Copy)
-        vs_col = [sb.tile([P, PACK], F32, name="vs_col%d" % a) for a in range(PASSES)]
+        kb_rows = {}
         for a in range(PASSES):
-            nc.scalar.dma_start(vs_col[a][:], vs_g[ROW:P, a * PASS : (a + 1) * PASS])
-
-        score_t = {}
-        for a in range(PASSES):
-            kw_g = sb.tile([P, PASS], U32, name="kw_g%d" % a, align_bytes=64)
-            nc.vector.tensor_copy(kw_g[:], listed(kw_pool[:].bitcast(U32), a))
-            for i in range(Q_TILES):
-                score_t[i, a] = bank(2 * i + a, "score_t%d%d" % (i, a))
-                for j in range(PACK):
-                    nc.tensor.matmul_mx(
-                        out=score_t[i, a][:, j * P : (j + 1) * P],
-                        lhsT=kw_g[:, j * P : (j + 1) * P].bitcast(FP8X4),
-                        lhsT_scale=ks_g[:, a * PASS + j * P : a * PASS + (j + 1) * P],
-                        rhs=q_codes[:, i * P : (i + 1) * P].bitcast(FP8X4),
-                        rhs_scale=q_scales[:, i * P : (i + 1) * P],
-                        start=True,
-                        stop=True,
-                    )
+            spread = bank(2 + a, "kb_spread%d" % a)
+            for j in range(PACK):
+                nc.tensor.transpose(spread[:, j * P : (j + 1) * P], kb_col[:, a, j : j + 1].to_broadcast([P, P]), ident[:])
+            kb_rows[a] = sb.tile([P, PACK, P], F32, name="kb_rows%d" % a)
+            nc.scalar.copy(kb_rows[a][:], spread[:].rearrange("q (s t) -> q t s", t=PACK))
 
         v_g = {}
-        for h in range(V_HALVES):
-            for a in range(PASSES):
-                if (h, a) != LAST:
-                    v_g[h, a] = sb.tile([P, PASS], BF16, name="v_g%d%d" % (h, a))
-                    nc.scalar.activation(v_g[h, a][:], listed(v_pool[h][:], a), ACT.Copy)
 
-        score = {}
-        for i in range(Q_TILES):
-            for a in range(PASSES):
-                biased = sb.tile([P, PACK, P], F32, name="biased%d%d" % (i, a))
-                nc.vector.tensor_tensor(
-                    biased[:],
-                    score_t[i, a][:].rearrange("s (j q) -> s j q", j=PACK),
-                    kb_col[:, a, :].unsqueeze(2).to_broadcast([P, PACK, P]),
-                    ALU.add,
-                )
-                score[i, a] = bank(4 + 2 * i + a, "score%d%d" % (i, a))
-                for j in range(PACK):
-                    nc.tensor.transpose(score[i, a][:, j * P : (j + 1) * P], biased[:, j, :], ident[:])
+        def gather_values(h, a, tag):
+            v_g[h, a] = sb.tile([P, PASS], BF16, name="v_g%d%d" % (h, a), tag=tag, align_bytes=64)
+            nc.scalar.activation(v_g[h, a][:], listed(v_pool[h][:], a), ACT.Copy)
 
-        weights, sums = [], []
+        gather_values(0, 0, "q_raw")
+        gather_values(0, 1, "v_g01")
+
+        least = {}
+
+        def add_scores(i, a):
+            raw = bank(4 + 2 * i + a, "raw%d%d" % (i, a))
+            nc.tensor.matmul_mx(
+                out=raw[:],
+                lhsT=q_codes[:, i * P : (i + 1) * P].bitcast(FP8X4),
+                lhsT_scale=q_scales[:, i * P : (i + 1) * P],
+                rhs=kw_g[a][:].bitcast(FP8X4),
+                rhs_scale=ks_g[:, a * PASS : (a + 1) * PASS],
+                start=True,
+                stop=True,
+            )
+            nc.vector.tensor_tensor(
+                score[i][:, a * PASS : (a + 1) * PASS].rearrange("q (t s) -> q t s", t=PACK),
+                raw[:].rearrange("q (s t) -> q t s", t=PACK),
+                kb_rows[a][:],
+                ALU.add,
+            )
+
+        def bound(i):
+            least[i] = sb.tile([P, 1], F32, name="least%d" % i, tag="least%d" % i, align_bytes=64)
+            nc.vector.tensor_reduce(least[i][:], score[i][:], mybir.AxisListType.X, ALU.max, negate=True)
+
+        add_scores(0, 0)
+        add_scores(0, 1)
+        add_scores(1, 0)
+        bound(0)
+        add_scores(1, 1)
+        bound(1)
+
+        weights = {}
+        part = sb.tile([P, PASSES, Q_TILES], F32, name="part")
         for i in range(Q_TILES):
-            neg = sb.tile([P, N + 1], F32, name="neg%d" % i)
-            nc.gpsimd.tensor_scalar(neg[:, N : N + 1], sink_col[:, i : i + 1], -1.0, 0.0, ALU.mult, ALU.add)
-            least = neg[:, N : N + 1]
-            for a in range(PASSES):
-                running = sb.tile([P, 1], F32, name="least%d%d" % (i, a), tag="least%d%d" % (i, a))
-                nc.vector.tensor_scalar(
-                    neg[:, a * PASS : (a + 1) * PASS].rearrange("q (t s) -> q t s", t=PACK),
-                    score[i, a][:].rearrange("q (s t) -> q t s", t=PACK),
-                    -1.0,
-                    least,
-                    ALU.mult,
-                    ALU.min,
-                    accum_out=running[:],
-                )
-                least = running[:]
-            p = sb.tile([P, N + 1], F32, name="p%d" % i)
-            part = sb.tile([P, PASSES], F32, name="part%d" % i)
+            if i == 1:
+                gather_values(1, 0, "v_g10")
+                gather_values(1, 1, "v_g11")
+            weights[i] = sb.tile([P, N + 1], F32, name="p%d" % i, tag="v_pool%d" % i)
             for a in range(PASSES):
                 cols = slice(a * PASS, (a + 1) * PASS + (1 if a == PASSES - 1 else 0))
-                nc.scalar.activation(p[:, cols], neg[:, cols], ACT.Exp, bias=least, scale=-1.0, accum_out=part[:, a : a + 1])
-            weights.append(p)
-            sums.append(part)
+                nc.scalar.activation(
+                    weights[i][:, cols], score[i][:, cols], ACT.Exp, bias=least[i][:], accum_out=part[:, a, i : i + 1]
+                )
 
-        v_g[LAST] = sb.tile([P, PASS], BF16, name="v_g_last", tag="least10")
-        nc.vector.tensor_copy(v_g[LAST][:], listed(v_pool[LAST[0]][:], LAST[1]))
+        v_codes, v_scales = {}, {}
 
-        v_codes, v_scales = [], []
-        for a in range(PASSES):
-            turned = bank(a, "v_turned%d" % a)
+        def quantize_values(a):
+            turned = bank(4 + a, "v_turned%d" % a)
             for h in range(V_HALVES):
                 words = v_g[h, a][:].bitcast(F32)
                 for u in range(2):
                     k = 2 * h + u
                     nc.tensor.transpose(turned[:, k * P : (k + 1) * P], words[:, u : 2 * P : 2], ident[:])
-            v_in = sb.tile([P, DV * PACK], BF16, name="v_in%d" % a, align_bytes=64)
+            v_in = sb.tile([P, DV * PACK], BF16, name="v_in%d" % a, tag=("score1", "least1")[a], align_bytes=64)
             nc.scalar.copy(
                 v_in[:].bitcast(F32).rearrange("s (h e u) -> s h e u", h=V_HALVES, u=2),
                 turned[:].rearrange("s (h u e) -> s h e u", h=V_HALVES, u=2),
             )
-            codes = sb.tile([P, DV], U32, name="v_codes%d" % a, align_bytes=64)
-            scales = sb.tile([P, DV], U8, name="v_scales%d" % a, align_bytes=64)
-            nc.vector.quantize_mx(out=codes[:].bitcast(FP8X4), scales=scales[:], in_=v_in[:])
-            v_codes.append(codes)
-            v_scales.append(scales)
+            v_codes[a] = sb.tile([P, DV], U32, name="v_codes%d" % a, align_bytes=64)
+            v_scales[a] = sb.tile([P, DV], U8, name="v_scales%d" % a, tag=("v_scales0", "vs_col1")[a], align_bytes=64)
+            nc.vector.quantize_mx(out=v_codes[a][:].bitcast(FP8X4), scales=v_scales[a][:], in_=v_in[:])
+
+        w_in, w_codes, w_scales = {}, {}, {}
+
+        def turn_and_scale(i, a):
+            turned = bank(2 * i + a, "p_turned%d%d" % (i, a))
+            for t in range(PACK):
+                c0 = a * PASS + t * P
+                nc.tensor.transpose(turned[:, t * P : (t + 1) * P], weights[i][:, c0 : c0 + P], ident[:])
+            w_in[i, a] = sb.tile([P, P, PACK], BF16, name="w_in%d%d" % (i, a), align_bytes=64)
+            nc.vector.tensor_tensor(
+                w_in[i, a][:],
+                turned[:].rearrange("s (t q) -> s q t", t=PACK),
+                vs_col[a][:].unsqueeze(1).to_broadcast([P, P, PACK]),
+                ALU.mult,
+            )
+
+        def quantize_weights(i, a):
+            w_codes[i, a] = sb.tile([P, P], U32, name="w_codes%d%d" % (i, a), align_bytes=64)
+            w_scales[i, a] = sb.tile([P, P], U8, name="w_scales%d%d" % (i, a), align_bytes=64)
+            nc.vector.quantize_mx(
+                out=w_codes[i, a][:].bitcast(FP8X4), scales=w_scales[i, a][:], in_=w_in[i, a][:].rearrange("s q t -> s (q t)")
+            )
+
+        for i in range(Q_TILES):
+            for a in range(PASSES):
+                turn_and_scale(i, a)
+            for a in range(PASSES):
+                quantize_weights(i, a)
+        for a in range(PASSES):
+            quantize_values(a)
+
+        total = sb.tile([P, Q_TILES], F32, name="total")
+        nc.vector.tensor_tensor(total[:], part[:, 0, :], part[:, 1, :], ALU.add)
+        inverse = sb.tile([P, Q_TILES], F32, name="inverse")
+        nc.vector.reciprocal(inverse[:], total[:])
 
         for i in range(Q_TILES):
             acc = bank(6 + i, "acc%d" % i)
             for a in range(PASSES):
-                turned = bank(2 + 2 * i + a, "p_turned%d%d" % (i, a))
-                for t in range(PACK):
-                    c0 = a * PASS + t * P
-                    nc.tensor.transpose(turned[:, t * P : (t + 1) * P], weights[i][:, c0 : c0 + P], ident[:])
-                w_in = sb.tile([P, P, PACK], BF16, name="w_in%d%d" % (i, a), align_bytes=64)
-                nc.vector.tensor_tensor(
-                    w_in[:],
-                    turned[:].rearrange("s (t q) -> s q t", t=PACK),
-                    vs_col[a][:].unsqueeze(1).to_broadcast([P, P, PACK]),
-                    ALU.mult,
-                )
-                w_codes = sb.tile([P, P], U32, name="w_codes%d%d" % (i, a), align_bytes=64)
-                w_scales = sb.tile([P, P], U8, name="w_scales%d%d" % (i, a), align_bytes=64)
-                nc.vector.quantize_mx(out=w_codes[:].bitcast(FP8X4), scales=w_scales[:], in_=w_in[:].rearrange("s q t -> s (q t)"))
                 nc.tensor.matmul_mx(
                     out=acc[:, 0:DV],
-                    lhsT=w_codes[:].bitcast(FP8X4),
-                    lhsT_scale=w_scales[:],
+                    lhsT=w_codes[i, a][:].bitcast(FP8X4),
+                    lhsT_scale=w_scales[i, a][:],
                     rhs=v_codes[a][:].bitcast(FP8X4),
                     rhs_scale=v_scales[a][:],
                     start=(a == 0),
                     stop=(a == PASSES - 1),
                 )
-            total = sb.tile([P, 1], F32, name="total%d" % i)
-            nc.vector.tensor_tensor(total[:], sums[i][:, 0:1], sums[i][:, 1:2], ALU.add)
-            inverse = sb.tile([P, 1], F32, name="inverse%d" % i)
-            nc.vector.reciprocal(inverse[:], total[:])
             result = sb.tile([P, DV], F32, name="result%d" % i)
-            nc.scalar.activation(result[:], acc[:, 0:DV], ACT.Copy, scale=inverse[:])
+            if i == 0:
+                nc.vector.tensor_scalar(result[:], acc[:, 0:DV], inverse[:, i : i + 1], None, ALU.mult)
+            else:
+                nc.scalar.activation(result[:], acc[:, 0:DV], ACT.Copy, scale=inverse[:, i : i + 1])
             nc.sync.dma_start(out[0, i * P : (i + 1) * P, :], result[:])

@@ -22,6 +22,7 @@ Q_TILES = NQ // P
 V_HALVES = DV // P
 COLS = PASS // 16
 ROW = P - 1
+PAD = 8
 
 FLOPS = 2 * NQ * N * D + 2 * NQ * N * DV
 BYTES = 4 * D * NQ + D * T + 16 * T + 4 * DV * T + 2 * 4 * T + 4 * NQ + 2 * P * N // 16 + 4 * NQ * DV
@@ -61,28 +62,38 @@ def tile_attend_soft_sink_kb_topkq256n1024t2048_kernel(tc, qT, k_words, k_scales
             )
         nc.sync.dma_start(kb_pool[ROW:P, :], kb[0:1, :])
         nc.sync.dma_start(vs_pool[ROW:P, :], vs[0:1, :])
-        kw_pool = sb.tile([P, T], I32, name="kw_pool", tag="kw_pool", align_bytes=64)
-        nc.sync.dma_start(kw_pool[:], k_words[0].rearrange("p n t -> p (n t)").bitcast(I32))
-        q_raw = sb.tile([P, PACK, NQ], F32, name="q_raw", tag="q_raw", align_bytes=64)
+        q_raw = sb.tile([P, PACK, NQ], F32, name="q_raw")
         nc.sync.dma_start(q_raw[:], qT[0].rearrange("(p j) w -> p j w", j=PACK))
-        score = [sb.tile([P, N + 1], F32, name="score%d" % i, tag="score%d" % i, align_bytes=64) for i in range(Q_TILES)]
-        for i in range(Q_TILES):
-            nc.sync.dma_start(score[i][:, N : N + 1], sink[0, i * P : (i + 1) * P, :])
+        kw_pool = sb.tile([P, T], I32, name="kw_pool", align_bytes=64)
+        nc.sync.dma_start(kw_pool[:], k_words[0].rearrange("p n t -> p (n t)").bitcast(I32))
+        sink_col = sb.tile([P, Q_TILES], F32, name="sink_col")
+        with nc.allow_non_contiguous_dma(reason="one sink a query row, one query row a partition"):
+            nc.sync.dma_start(sink_col[:], sink[0].rearrange("(i p) o -> p (i o)", p=P))
         v_pool = [sb.tile([P, T], F32, name="v_pool%d" % h, tag="v_pool%d" % h) for h in range(V_HALVES)]
         for h in range(V_HALVES):
             nc.sync.dma_start(v_pool[h][:], vT[h * P : (h + 1) * P, :])
 
-
         ks_g = sb.tile([P, N], U8, name="ks_g", align_bytes=64)
         nc.vector.tensor_copy(ks_g[:], ks_pool[:].indirect(offsets[:]))
 
-        kb_turned = {}
+        q_in = sb.tile([P, NQ, PACK], BF16, name="q_in", align_bytes=64)
+        nc.vector.tensor_copy(
+            q_in[:].rearrange("p (c i) t -> p c t i", i=4),
+            q_raw[:].rearrange("p t (c i) -> p c t i", i=4),
+        )
+
+        kb_col = sb.tile([P, PASSES, PACK], F32, name="kb_col")
         for a in range(PASSES):
             kb_g = sb.tile([P, PASS], F32, name="kb_g%d" % a, tag="kb_g%d" % a)
             nc.scalar.activation(kb_g[:], listed(kb_pool[:], a), ACT.Copy)
-            kb_turned[a] = bank(a, "kb_turned%d" % a)
+            turned = bank(4 + a, "kb_turned%d" % a)
             for j in range(PACK):
-                nc.tensor.transpose(kb_turned[a][:, j * P : (j + 1) * P], kb_g[:, j * P : (j + 1) * P], ident[:])
+                nc.tensor.transpose(turned[:, j * P : (j + 1) * P], kb_g[:, j * P : (j + 1) * P], ident[:])
+            nc.vector.tensor_copy(kb_col[:, a, :], turned[:, ROW:PASS:P])
+
+        q_codes = sb.tile([P, NQ], U32, name="q_codes", align_bytes=64)
+        q_scales = sb.tile([P, NQ], U8, name="q_scales", align_bytes=64)
+        nc.vector.quantize_mx(out=q_codes[:].bitcast(FP8X4), scales=q_scales[:], in_=q_in[:].rearrange("p w t -> p (w t)"))
 
         vs_g = sb.tile([P, N], F32, name="vs_g", tag="kb_g0")
         nc.scalar.activation(vs_g[:], vs_pool[:].indirect(offsets[:]), ACT.Copy)
@@ -91,98 +102,82 @@ def tile_attend_soft_sink_kb_topkq256n1024t2048_kernel(tc, qT, k_words, k_scales
             vs_col[a] = sb.tile([P, PACK], F32, name="vs_col%d" % a, tag="vs_col%d" % a, align_bytes=64)
             nc.sync.dma_start(vs_col[a][:], vs_g[ROW:P, a * PASS : (a + 1) * PASS])
 
-        kw_g = {}
-
-        def gather_keys(a, tag):
-            kw_g[a] = sb.tile([P, PASS], U32, name="kw_g%d" % a, tag=tag, align_bytes=64)
-            nc.vector.tensor_copy(kw_g[a][:], listed(kw_pool[:].bitcast(U32), a))
-
-        gather_keys(0, "kw_g0")
-        q_in = sb.tile([P, NQ, PACK], BF16, name="q_in", tag="q_in", align_bytes=64)
-        nc.vector.tensor_copy(
-            q_in[:].rearrange("p (c i) t -> p c t i", i=4),
-            q_raw[:].rearrange("p t (c i) -> p c t i", i=4),
-        )
-        kb_col = sb.tile([P, PASSES, PACK], F32, name="kb_col", tag="q_raw", align_bytes=64)
+        score_t = {}
         for a in range(PASSES):
-            nc.vector.tensor_copy(kb_col[:, a, :], kb_turned[a][:, ROW:PASS:P])
-        q_codes = sb.tile([P, NQ], U32, name="q_codes", align_bytes=64)
-        q_scales = sb.tile([P, NQ], U8, name="q_scales", align_bytes=64)
-        nc.vector.quantize_mx(out=q_codes[:].bitcast(FP8X4), scales=q_scales[:], in_=q_in[:].rearrange("p w t -> p (w t)"))
-        gather_keys(1, "q_in")
-
-        kb_rows = {}
-        for a in range(PASSES):
-            spread = bank(2 + a, "kb_spread%d" % a)
-            for j in range(PACK):
-                nc.tensor.transpose(spread[:, j * P : (j + 1) * P], kb_col[:, a, j : j + 1].to_broadcast([P, P]), ident[:])
-            kb_rows[a] = sb.tile([P, PACK, P], F32, name="kb_rows%d" % a)
-            nc.scalar.copy(kb_rows[a][:], spread[:].rearrange("q (s t) -> q t s", t=PACK))
+            kw_g = sb.tile([P, PASS], U32, name="kw_g%d" % a, align_bytes=64)
+            nc.vector.tensor_copy(kw_g[:], listed(kw_pool[:].bitcast(U32), a))
+            for i in range(Q_TILES):
+                score_t[i, a] = bank(2 * i + a, "score_t%d%d" % (i, a))
+                for j in range(PACK):
+                    nc.tensor.matmul_mx(
+                        out=score_t[i, a][:, j * P : (j + 1) * P],
+                        lhsT=kw_g[:, j * P : (j + 1) * P].bitcast(FP8X4),
+                        lhsT_scale=ks_g[:, a * PASS + j * P : a * PASS + (j + 1) * P],
+                        rhs=q_codes[:, i * P : (i + 1) * P].bitcast(FP8X4),
+                        rhs_scale=q_scales[:, i * P : (i + 1) * P],
+                        start=True,
+                        stop=True,
+                    )
 
         v_g = {}
+        for h in range(V_HALVES):
+            for a in range(PASSES):
+                v_g[h, a] = sb.tile([P, PASS], BF16, name="v_g%d%d" % (h, a))
+                nc.scalar.activation(v_g[h, a][:], listed(v_pool[h][:], a), ACT.Copy)
 
-        def gather_values(h, a, tag):
-            v_g[h, a] = sb.tile([P, PASS], BF16, name="v_g%d%d" % (h, a), tag=tag, align_bytes=64)
-            nc.scalar.activation(v_g[h, a][:], listed(v_pool[h][:], a), ACT.Copy)
+        neg, least, score = {}, {}, {}
+        for i in range(Q_TILES):
+            neg[i] = sb.tile([P, N + 1], F32, name="neg%d" % i, tag="neg%d" % i, align_bytes=64)
+            nc.gpsimd.tensor_scalar(neg[i][:, N : N + 1], sink_col[:, i : i + 1], -1.0, 0.0, ALU.mult, ALU.add)
+            least[i] = neg[i][:, N : N + 1]
 
-        gather_values(0, 0, "q_raw")
-        gather_values(0, 1, "v_g01")
+        for a in range(PASSES):
+            for i in range(Q_TILES):
+                biased = sb.tile([P, PACK, P], F32, name="biased%d%d" % (i, a))
+                nc.vector.tensor_tensor(
+                    biased[:],
+                    score_t[i, a][:].rearrange("s (j q) -> s j q", j=PACK),
+                    kb_col[:, a, :].unsqueeze(2).to_broadcast([P, PACK, P]),
+                    ALU.add,
+                )
+                score[i, a] = bank(4 + 2 * i + a, "score%d%d" % (i, a))
+                for j in range(PACK):
+                    nc.tensor.transpose(score[i, a][:, j * P : (j + 1) * P], biased[:, j, :], ident[:])
 
-        least = {}
+        for a in range(PASSES):
+            for i in range(Q_TILES):
+                running = sb.tile([P, 1], F32, name="least%d%d" % (i, a))
+                nc.vector.tensor_scalar(
+                    neg[i][:, a * PASS : (a + 1) * PASS].rearrange("q (t s) -> q t s", t=PACK),
+                    score[i, a][:].rearrange("q (s t) -> q t s", t=PACK),
+                    -1.0,
+                    least[i],
+                    ALU.mult,
+                    ALU.min,
+                    accum_out=running[:],
+                )
+                least[i] = running[:]
 
-        def add_scores(i, a):
-            raw = bank(4 + 2 * i + a, "raw%d%d" % (i, a))
-            nc.tensor.matmul_mx(
-                out=raw[:],
-                lhsT=q_codes[:, i * P : (i + 1) * P].bitcast(FP8X4),
-                lhsT_scale=q_scales[:, i * P : (i + 1) * P],
-                rhs=kw_g[a][:].bitcast(FP8X4),
-                rhs_scale=ks_g[:, a * PASS : (a + 1) * PASS],
-                start=True,
-                stop=True,
-            )
-            nc.vector.tensor_tensor(
-                score[i][:, a * PASS : (a + 1) * PASS].rearrange("q (t s) -> q t s", t=PACK),
-                raw[:].rearrange("q (s t) -> q t s", t=PACK),
-                kb_rows[a][:],
-                ALU.add,
-            )
-
-        def bound(i):
-            least[i] = sb.tile([P, 1], F32, name="least%d" % i, tag="least%d" % i, align_bytes=64)
-            nc.vector.tensor_reduce(least[i][:], score[i][:], mybir.AxisListType.X, ALU.max, negate=True)
-
-        add_scores(0, 0)
-        add_scores(0, 1)
-        add_scores(1, 0)
-        bound(0)
-        add_scores(1, 1)
-        bound(1)
-
-        weights = {}
+        weights = sb.tile([P, Q_TILES, N + PAD], F32, name="weights", tag="v_pool1")
         part = sb.tile([P, PASSES, Q_TILES], F32, name="part")
         for i in range(Q_TILES):
-            if i == 1:
-                gather_values(1, 0, "v_g10")
-                gather_values(1, 1, "v_g11")
-            weights[i] = sb.tile([P, N + 1], F32, name="p%d" % i, tag="v_pool%d" % i)
             for a in range(PASSES):
                 cols = slice(a * PASS, (a + 1) * PASS + (1 if a == PASSES - 1 else 0))
                 nc.scalar.activation(
-                    weights[i][:, cols], score[i][:, cols], ACT.Exp, bias=least[i][:], accum_out=part[:, a, i : i + 1]
+                    weights[:, i, cols], neg[i][:, cols], ACT.Exp, bias=least[i], scale=-1.0, accum_out=part[:, a, i : i + 1]
                 )
 
         v_codes, v_scales = {}, {}
 
         def quantize_values(a):
-            turned = bank(4 + a, "v_turned%d" % a)
+            turned = bank(a, "v_turned%d" % a)
             for h in range(V_HALVES):
                 words = v_g[h, a][:].bitcast(F32)
                 for u in range(2):
                     k = 2 * h + u
                     nc.tensor.transpose(turned[:, k * P : (k + 1) * P], words[:, u : 2 * P : 2], ident[:])
-            v_in = sb.tile([P, DV * PACK], BF16, name="v_in%d" % a, tag=("score1", "least1")[a], align_bytes=64)
-            nc.scalar.copy(
+            v_in = sb.tile([P, DV * PACK], BF16, name="v_in%d" % a, tag=("v_in0", "neg1")[a], align_bytes=64)
+            (nc.vector.tensor_copy, nc.scalar.copy)[a](
                 v_in[:].bitcast(F32).rearrange("s (h e u) -> s h e u", h=V_HALVES, u=2),
                 turned[:].rearrange("s (h u e) -> s h e u", h=V_HALVES, u=2),
             )
@@ -193,10 +188,10 @@ def tile_attend_soft_sink_kb_topkq256n1024t2048_kernel(tc, qT, k_words, k_scales
         w_in, w_codes, w_scales = {}, {}, {}
 
         def turn_and_scale(i, a):
-            turned = bank(2 * i + a, "p_turned%d%d" % (i, a))
+            turned = bank(2 + 2 * i + a, "p_turned%d%d" % (i, a))
             for t in range(PACK):
                 c0 = a * PASS + t * P
-                nc.tensor.transpose(turned[:, t * P : (t + 1) * P], weights[i][:, c0 : c0 + P], ident[:])
+                nc.tensor.transpose(turned[:, t * P : (t + 1) * P], weights[:, i, c0 : c0 + P], ident[:])
             w_in[i, a] = sb.tile([P, P, PACK], BF16, name="w_in%d%d" % (i, a), align_bytes=64)
             nc.vector.tensor_tensor(
                 w_in[i, a][:],
@@ -212,13 +207,14 @@ def tile_attend_soft_sink_kb_topkq256n1024t2048_kernel(tc, qT, k_words, k_scales
                 out=w_codes[i, a][:].bitcast(FP8X4), scales=w_scales[i, a][:], in_=w_in[i, a][:].rearrange("s q t -> s (q t)")
             )
 
+        quantize_values(0)
         for i in range(Q_TILES):
             for a in range(PASSES):
                 turn_and_scale(i, a)
+            if i == Q_TILES - 1:
+                quantize_values(1)
             for a in range(PASSES):
                 quantize_weights(i, a)
-        for a in range(PASSES):
-            quantize_values(a)
 
         total = sb.tile([P, Q_TILES], F32, name="total")
         nc.vector.tensor_tensor(total[:], part[:, 0, :], part[:, 1, :], ALU.add)
@@ -238,8 +234,5 @@ def tile_attend_soft_sink_kb_topkq256n1024t2048_kernel(tc, qT, k_words, k_scales
                     stop=(a == PASSES - 1),
                 )
             result = sb.tile([P, DV], F32, name="result%d" % i)
-            if i == 0:
-                nc.vector.tensor_scalar(result[:], acc[:, 0:DV], inverse[:, i : i + 1], None, ALU.mult)
-            else:
-                nc.scalar.activation(result[:], acc[:, 0:DV], ACT.Copy, scale=inverse[:, i : i + 1])
+            nc.scalar.activation(result[:], acc[:, 0:DV], ACT.Copy, scale=inverse[:, i : i + 1])
             nc.sync.dma_start(out[0, i * P : (i + 1) * P, :], result[:])

from contextlib import ExitStack

import concourse.mybir as mybir
from concourse.masks import make_identity

F32 = mybir.dt.float32
BF16 = mybir.dt.bfloat16
I32 = mybir.dt.int32
U32 = mybir.dt.uint32
U16 = mybir.dt.uint16
U8 = mybir.dt.uint8
FP8X4 = mybir.dt.float8_e4m3fn_x4
ALU = mybir.AluOpType
ACT = mybir.ActivationFunctionType

P = 128
PACK = 4
PASS = P * PACK
N, T, D, DV, NQ = 1024, 2048, 512, 256, 256
PASSES = N // PASS
Q_TILES = NQ // P
V_HALVES = DV // P
COLS = PASS // 16
ROW = P - 1
PAD = 8

FLOPS = 2 * NQ * N * D + 2 * NQ * N * DV
BYTES = 4 * D * NQ + D * T + 16 * T + 4 * DV * T + 2 * 4 * T + 4 * NQ + 2 * P * N // 16 + 4 * NQ * DV


def tile_attend_soft_sink_kb_topkq256n1024t2048_kernel(tc, qT, k_words, k_scales, vT, vs, kb, sink, offs, out):
    nc = tc.nc
    with ExitStack() as ctx:
        sb = ctx.enter_context(tc.tile_pool(name="sb", bufs=1))
        ps = ctx.enter_context(tc.psum_pool(name="ps", bufs=1))

        def bank(b, name):
            return ps.tile([P, PASS], F32, name=name, tag="bank%d" % b)

        warm = sb.tile([P, 2], F32, name="warm")
        nc.gpsimd.memset(warm[:, 0:1], 0.0)
        nc.scalar.activation(warm[:, 1:2], warm[:, 0:1], ACT.Exp)
        ident = sb.tile([P, P], F32, name="ident")
        make_identity(nc, ident[:])

        offsets = sb.tile([P, N // 16], U16, name="offsets")
        nc.sync.dma_start(offsets[:], offs)

        def listed(window, a):
            return window.indirect(offsets[:, a * COLS : (a + 1) * COLS])

        ks_pool = sb.tile([P, T], U8, name="ks_pool", align_bytes=64)
        kb_pool = sb.tile([P, T], F32, name="kb_pool")
        vs_pool = sb.tile([P, T], F32, name="vs_pool")
        nc.vector.memset(kb_pool[0:ROW, 0 : T // 2 - 1], 0.0)
        nc.vector.memset(kb_pool[0:ROW, T // 2 - 1 : T], 0.0)
        nc.gpsimd.memset(vs_pool[0:ROW, :], 0.0)
        for quad in range(4):
            nc.sync.dma_start(
                ks_pool[32 * quad : 32 * (quad + 1), :].bitcast(I32),
                k_scales[0, 4 * quad : 4 * quad + 4, :].bitcast(I32).unsqueeze(0).to_broadcast([8, 4, T // 4]),
            )
        nc.sync.dma_start(kb_pool[ROW:P, :], kb[0:1, :])
        nc.sync.dma_start(vs_pool[ROW:P, :], vs[0:1, :])
        q_raw = sb.tile([P, PACK, NQ], F32, name="q_raw")
        nc.sync.dma_start(q_raw[:], qT[0].rearrange("(p j) w -> p j w", j=PACK))
        kw_pool = sb.tile([P, T], I32, name="kw_pool", align_bytes=64)
        nc.sync.dma_start(kw_pool[:], k_words[0].rearrange("p n t -> p (n t)").bitcast(I32))
        sink_col = sb.tile([P, Q_TILES], F32, name="sink_col")
        with nc.allow_non_contiguous_dma(reason="one sink a query row, one query row a partition"):
            nc.sync.dma_start(sink_col[:], sink[0].rearrange("(i p) o -> p (i o)", p=P))
        v_pool = [sb.tile([P, T], F32, name="v_pool%d" % h, tag="v_pool%d" % h) for h in range(V_HALVES)]
        for h in range(V_HALVES):
            nc.sync.dma_start(v_pool[h][:], vT[h * P : (h + 1) * P, :])

        ks_g = sb.tile([P, N], U8, name="ks_g", align_bytes=64)
        nc.vector.tensor_copy(ks_g[:], ks_pool[:].indirect(offsets[:]))

        q_in = sb.tile([P, NQ, PACK], BF16, name="q_in", align_bytes=64)
        nc.vector.tensor_copy(
            q_in[:].rearrange("p (c i) t -> p c t i", i=4),
            q_raw[:].rearrange("p t (c i) -> p c t i", i=4),
        )

        kb_col = sb.tile([P, PASSES, PACK], F32, name="kb_col")
        for a in range(PASSES):
            kb_g = sb.tile([P, PASS], F32, name="kb_g%d" % a, tag="kb_g%d" % a)
            nc.scalar.activation(kb_g[:], listed(kb_pool[:], a), ACT.Copy)
            turned = bank(4 + a, "kb_turned%d" % a)
            for j in range(PACK):
                nc.tensor.transpose(turned[:, j * P : (j + 1) * P], kb_g[:, j * P : (j + 1) * P], ident[:])
            nc.vector.tensor_copy(kb_col[:, a, :], turned[:, ROW:PASS:P])

        q_codes = sb.tile([P, NQ], U32, name="q_codes", align_bytes=64)
        q_scales = sb.tile([P, NQ], U8, name="q_scales", align_bytes=64)
        nc.vector.quantize_mx(out=q_codes[:].bitcast(FP8X4), scales=q_scales[:], in_=q_in[:].rearrange("p w t -> p (w t)"))

        vs_g = sb.tile([P, N], F32, name="vs_g", tag="kb_g0")
        nc.scalar.activation(vs_g[:], vs_pool[:].indirect(offsets[:]), ACT.Copy)
        vs_col = {}
        for a in range(PASSES):
            vs_col[a] = sb.tile([P, PACK], F32, name="vs_col%d" % a, tag="vs_col%d" % a, align_bytes=64)
            nc.sync.dma_start(vs_col[a][:], vs_g[ROW:P, a * PASS : (a + 1) * PASS])

        score_t = {}
        for a in range(PASSES):
            kw_g = sb.tile([P, PASS], U32, name="kw_g%d" % a, align_bytes=64)
            nc.vector.tensor_copy(kw_g[:], listed(kw_pool[:].bitcast(U32), a))
            for i in range(Q_TILES):
                score_t[i, a] = bank(2 * i + a, "score_t%d%d" % (i, a))
                for j in range(PACK):
                    nc.tensor.matmul_mx(
                        out=score_t[i, a][:, j * P : (j + 1) * P],
                        lhsT=kw_g[:, j * P : (j + 1) * P].bitcast(FP8X4),
                        lhsT_scale=ks_g[:, a * PASS + j * P : a * PASS + (j + 1) * P],
                        rhs=q_codes[:, i * P : (i + 1) * P].bitcast(FP8X4),
                        rhs_scale=q_scales[:, i * P : (i + 1) * P],
                        start=True,
                        stop=True,
                    )

        v_g = {}
        for h in range(V_HALVES):
            for a in range(PASSES):
                v_g[h, a] = sb.tile([P, PASS], BF16, name="v_g%d%d" % (h, a))
                nc.scalar.activation(v_g[h, a][:], listed(v_pool[h][:], a), ACT.Copy)

        neg, least, score = {}, {}, {}
        for i in range(Q_TILES):
            neg[i] = sb.tile([P, N + 1], F32, name="neg%d" % i, tag="neg%d" % i, align_bytes=64)
            nc.gpsimd.tensor_scalar(neg[i][:, N : N + 1], sink_col[:, i : i + 1], -1.0, 0.0, ALU.mult, ALU.add)
            least[i] = neg[i][:, N : N + 1]

        for a in range(PASSES):
            for i in range(Q_TILES):
                biased = sb.tile([P, PACK, P], F32, name="biased%d%d" % (i, a))
                nc.vector.tensor_tensor(
                    biased[:],
                    score_t[i, a][:].rearrange("s (j q) -> s j q", j=PACK),
                    kb_col[:, a, :].unsqueeze(2).to_broadcast([P, PACK, P]),
                    ALU.add,
                )
                score[i, a] = bank(4 + 2 * i + a, "score%d%d" % (i, a))
                for j in range(PACK):
                    nc.tensor.transpose(score[i, a][:, j * P : (j + 1) * P], biased[:, j, :], ident[:])

        for a in range(PASSES):
            for i in range(Q_TILES):
                running = sb.tile([P, 1], F32, name="least%d%d" % (i, a))
                nc.vector.tensor_scalar(
                    neg[i][:, a * PASS : (a + 1) * PASS].rearrange("q (t s) -> q t s", t=PACK),
                    score[i, a][:].rearrange("q (s t) -> q t s", t=PACK),
                    -1.0,
                    least[i],
                    ALU.mult,
                    ALU.min,
                    accum_out=running[:],
                )
                least[i] = running[:]

        weights = sb.tile([P, Q_TILES, N + PAD], F32, name="weights", tag="v_pool1")
        part = sb.tile([P, PASSES, Q_TILES], F32, name="part")
        for i in range(Q_TILES):
            for a in range(PASSES):
                cols = slice(a * PASS, (a + 1) * PASS + (1 if a == PASSES - 1 else 0))
                nc.scalar.activation(
                    weights[:, i, cols], neg[i][:, cols], ACT.Exp, bias=least[i], scale=-1.0, accum_out=part[:, a, i : i + 1]
                )

        v_codes, v_scales = {}, {}

        def quantize_values(a):
            turned = bank(a, "v_turned%d" % a)
            for h in range(V_HALVES):
                words = v_g[h, a][:].bitcast(F32)
                for u in range(2):
                    k = 2 * h + u
                    nc.tensor.transpose(turned[:, k * P : (k + 1) * P], words[:, u : 2 * P : 2], ident[:])
            v_in = sb.tile([P, DV * PACK], BF16, name="v_in%d" % a, tag=("v_in0", "neg1")[a], align_bytes=64)
            (nc.vector.tensor_copy, nc.scalar.copy)[a](
                v_in[:].bitcast(F32).rearrange("s (h e u) -> s h e u", h=V_HALVES, u=2),
                turned[:].rearrange("s (h u e) -> s h e u", h=V_HALVES, u=2),
            )
            v_codes[a] = sb.tile([P, DV], U32, name="v_codes%d" % a, align_bytes=64)
            v_scales[a] = sb.tile([P, DV], U8, name="v_scales%d" % a, tag=("v_scales0", "vs_col1")[a], align_bytes=64)
            nc.vector.quantize_mx(out=v_codes[a][:].bitcast(FP8X4), scales=v_scales[a][:], in_=v_in[:])

        w_in, w_codes, w_scales = {}, {}, {}

        def turn_and_scale(i, a):
            turned = bank(2 + 2 * i + a, "p_turned%d%d" % (i, a))
            for t in range(PACK):
                c0 = a * PASS + t * P
                nc.tensor.transpose(turned[:, t * P : (t + 1) * P], weights[:, i, c0 : c0 + P], ident[:])
            w_in[i, a] = sb.tile([P, P, PACK], BF16, name="w_in%d%d" % (i, a), align_bytes=64)
            nc.vector.tensor_tensor(
                w_in[i, a][:],
                turned[:].rearrange("s (t q) -> s q t", t=PACK),
                vs_col[a][:].unsqueeze(1).to_broadcast([P, P, PACK]),
                ALU.mult,
            )

        def quantize_weights(i, a):
            w_codes[i, a] = sb.tile([P, P], U32, name="w_codes%d%d" % (i, a), align_bytes=64)
            w_scales[i, a] = sb.tile([P, P], U8, name="w_scales%d%d" % (i, a), align_bytes=64)
            nc.vector.quantize_mx(
                out=w_codes[i, a][:].bitcast(FP8X4), scales=w_scales[i, a][:], in_=w_in[i, a][:].rearrange("s q t -> s (q t)")
            )

        quantize_values(0)
        for i in range(Q_TILES):
            for a in range(PASSES):
                turn_and_scale(i, a)
            if i == Q_TILES - 1:
                quantize_values(1)
            for a in range(PASSES):
                quantize_weights(i, a)

        total = sb.tile([P, Q_TILES], F32, name="total")
        nc.vector.tensor_tensor(total[:], part[:, 0, :], part[:, 1, :], ALU.add)
        inverse = sb.tile([P, Q_TILES], F32, name="inverse")
        nc.vector.reciprocal(inverse[:], total[:])

        for i in range(Q_TILES):
            acc = bank(6 + i, "acc%d" % i)
            for a in range(PASSES):
                nc.tensor.matmul_mx(
                    out=acc[:, 0:DV],
                    lhsT=w_codes[i, a][:].bitcast(FP8X4),
                    lhsT_scale=w_scales[i, a][:],
                    rhs=v_codes[a][:].bitcast(FP8X4),
                    rhs_scale=v_scales[a][:],
                    start=(a == 0),
                    stop=(a == PASSES - 1),
                )
            result = sb.tile([P, DV], F32, name="result%d" % i)
            nc.scalar.activation(result[:], acc[:, 0:DV], ACT.Copy, scale=inverse[:, i : i + 1])
            nc.sync.dma_start(out[0, i * P : (i + 1) * P, :], result[:])
